import numpy as np
import ml_dtypes


def mxq(x, axis, fmt="e4m3"):
    dtype, down = {"e4m3": (ml_dtypes.float8_e4m3fn, 7), "e5m2": (ml_dtypes.float8_e5m2, 14)}[fmt]
    v = np.moveaxis(np.asarray(x, np.float32).astype(ml_dtypes.bfloat16).astype(np.float64), axis, -1)
    blocks = v.reshape(v.shape[:-1] + (-1, 32))
    amax = np.abs(blocks).max(-1, keepdims=True)
    byte = np.maximum(np.where(amax > 0, np.frexp(amax)[1] - 1 + 127, 0) - down, 1)
    scale = np.exp2(byte - 127.0)
    codes = (blocks / scale).astype(np.float32).astype(dtype).astype(np.float64)
    return np.moveaxis((codes * scale).reshape(v.shape), -1, axis)


WIDE = False


def mx_kscale(k):
    if not WIDE:
        return np.ones(k)
    levels = np.array([10, -10, 5, -5, 0])
    if k % 512:
        return np.exp2(np.random.permutation(np.resize(levels, k // 32))).repeat(32)
    a = np.empty((k // 512, 16))
    for p in range(k // 512):
        a[p, :8] = np.random.permutation(np.resize(levels, 8))
        for g in range(8):
            far = levels[np.abs(levels - a[p, g]) >= 10]
            a[p, g + 8] = far[np.random.randint(len(far))]
    return np.exp2(a.ravel()).repeat(32)


def f64(x):
    return np.asarray(x).astype(np.float64)


def striped(idx):
    return np.tile(idx.reshape(-1, 16).T, (8, 1)).astype(np.uint16)


def unstriped(offs):
    return offs[:16].T.reshape(-1).astype(np.int64)


E2M1 = np.array([0.0, 0.5, 1.0, 1.5, 2.0, 3.0, 4.0, 6.0, -0.0, -0.5, -1.0, -1.5, -2.0, -3.0, -4.0, -6.0])


def pack_weight(w, fmt):
    k, n = w.shape
    w = f64(np.asarray(w, np.float32).astype(ml_dtypes.bfloat16)).reshape(k // 32, 32, n)
    amax = np.abs(w).max(1)
    if fmt == "e4m3":
        byte = np.frexp(amax)[1] - 1 + 127 - 7
    else:
        mant, ex = np.frexp(amax / 6.0)
        byte = np.where(mant > 0.5, ex, ex - 1) + 127
    byte = np.clip(np.where(amax > 0, byte, 1), 1, 254)
    scaled = (w * np.exp2(127.0 - byte)[:, None, :]).reshape(k, n).astype(np.float32)
    by_word = np.ascontiguousarray(scaled.reshape(k // 512, 128, 4, n).transpose(0, 1, 3, 2))
    if fmt == "e4m3":
        words = by_word.astype(ml_dtypes.float8_e4m3fn).view(np.uint8)
    else:
        c = by_word.astype(ml_dtypes.float4_e2m1fn).view(np.uint8) & 0xF
        words = (c[..., 0::2] | (c[..., 1::2] << 4)).reshape(k // 512, 128, 2 * n)
    return np.ascontiguousarray(words), np.ascontiguousarray(byte.astype(np.uint8).reshape(k // 512, 16, n))


def unpack_weight(words, scales, fmt):
    g, _, n = scales.shape
    words = np.ascontiguousarray(words).reshape(g, 128, n, -1)
    if fmt == "e4m3":
        vals = words.view(ml_dtypes.float8_e4m3fn).astype(np.float64)
    else:
        nib = np.empty((g, 128, n, 4), np.uint8)
        nib[..., 0::2] = words & 0xF
        nib[..., 1::2] = words >> 4
        vals = E2M1[nib]
    vals = vals * np.repeat(np.exp2(scales.astype(np.float64) - 127.0), 8, axis=1)[..., None]
    return vals.transpose(0, 1, 3, 2).reshape(g * 512, n)


def gelu(v):
    return 0.5 * v * (1.0 + np.tanh(np.sqrt(2.0 / np.pi) * (v + 0.044715 * v**3)))


K, H, T, S, T3, S2, T2 = 1024, 1024, 2048, 512, 2048, 512, 1024

def setup_inputs():
    n = np.random.standard_normal
    s = mx_kscale(K)[:, None]
    u = s
    tab_words, tab_scales = pack_weight(n((K, T)) * s, "e4m3")
    tab2_words, tab2_scales = pack_weight(n((H, T3)) / np.sqrt(H) / u, "e4m3")
    w4_words, w4_scales = pack_weight(n((K, H)) / np.sqrt(K) / s * u.T, "e2m1")
    return {
        "tab_words": tab_words, "tab_scales": tab_scales,
        "offs": striped(np.random.permutation(T)[:S]),
        "tab2_words": tab2_words, "tab2_scales": tab2_scales,
        "offs2": striped(np.random.permutation(T3)[:S2]),
        "offs3": striped(np.random.permutation(T2)[:S]),
        "w1": (n((K, H)) / np.sqrt(K) / s * u.T).astype(np.float32),
        "w4_words": w4_words, "w4_scales": w4_scales,
        "seen": (n((H, S)) * u).astype(np.float32),
        "ba": (0.8 * n(S2)).astype(np.float32),
        "bt": (0.8 * n(S2)).astype(np.float32),
        "wgo": np.exp(0.3 * n((128, S))).astype(np.float32),
        "page1": n((S2, T2)).astype(np.float32),
    }

def reference(tab_words, tab_scales, offs, tab2_words, tab2_scales, offs2, offs3,
              w1, w4_words, w4_scales, seen, ba, bt, wgo, page1):
    v = unpack_weight(tab_words, tab_scales, "e4m3")[:, unstriped(offs)]
    v2 = unpack_weight(tab2_words, tab2_scales, "e4m3")[:, unstriped(offs2)]
    w1q = mxq(f64(w1), 0, "e4m3")
    w4 = unpack_weight(w4_words, w4_scales, "e2m1")
    h = np.maximum(w1q.T @ v, f64(seen)) + (w4.T @ v)
    hq = mxq(h, 0, "e4m3")
    e = (v2.T @ hq) + f64(ba)[:, None]
    d = (v2.T @ v) + f64(bt)[:, None]
    y = e * np.tanh(d)
    out = f64(page1).copy()
    out[:, unstriped(offs3)] = np.tile(f64(wgo), (S2 // 128, 1)) * y
    return out

@@ -1,0 +1,211 @@
+from contextlib import ExitStack
+
+import concourse.mybir as mybir
+
+K, H, T, S, T3, S2, T2 = 1024, 1024, 2048, 512, 2048, 512, 1024
+FLOPS = 2 * (2 * K * H * S + 2 * H * S2 * S)
+
+F32 = mybir.dt.float32
+BF16 = mybir.dt.bfloat16
+I32 = mybir.dt.int32
+U32 = mybir.dt.uint32
+U16 = mybir.dt.uint16
+U8 = mybir.dt.uint8
+FP8X4 = mybir.dt.float8_e4m3fn_x4
+FP4X4 = mybir.dt.float4_e2m1fn_x4
+ALU = mybir.AluOpType
+ACT = mybir.ActivationFunctionType
+
+P = 128
+PACK = 4
+KP = P * PACK
+NPASS = K // KP
+NBLK = H // KP
+MT = S2 // P
+JQ = S // P
+
+
+def tile_list_derby_jam_lineups_kernel(tc, tab_words, tab_scales, offs, tab2_words, tab2_scales, offs2, offs3,
+                                                 w1, w4_words, w4_scales, seen, ba, bt, wgo, page1, out):
+    nc = tc.nc
+    with ExitStack() as ctx:
+        keep = ctx.enter_context(tc.tile_pool(name="keep", bufs=1))
+        psum = ctx.enter_context(tc.psum_pool(name="psum", bufs=4))
+
+        def held(name, shape, dtype):
+            return keep.tile(shape, dtype, name=name, align_bytes=64)
+
+        idx = keep.tile([P, S // 16], U16, name="idx")
+        idx2 = keep.tile([P, S2 // 16], U16, name="idx2")
+        idx3 = keep.tile([P, S // 16], U16, name="idx3")
+        tab = [held("tab%d" % a, [P, T], I32) for a in range(NPASS)]
+        tab2 = [held("tab2_%d" % a, [P, T3], I32) for a in range(NPASS)]
+        tab_sc = held("tab_sc", [P, NPASS * T], U8)
+        tab2_sc = held("tab2_sc", [P, T3], U8)
+        w4_raw = held("w4_raw", [P, NPASS * 2 * H], U8)
+        w4_sc_raw = held("w4_sc_raw", [P, NPASS * H], U8)
+        w4 = held("w4", [P, NPASS * 2 * H], U8)
+        w4_sc = held("w4_sc", [P, NPASS * H], U8)
+        w1_raw = [[held("w1_raw%d%d" % (b, a), [P, PACK, KP], F32) for a in range(NPASS)] for b in range(NBLK)]
+        w1_bf = [[held("w1_bf%d%d" % (b, a), [P, KP * PACK], BF16) for a in range(NPASS)] for b in range(NBLK)]
+        w1_q = [[held("w1_q%d%d" % (b, a), [P, KP], U32) for a in range(NPASS)] for b in range(NBLK)]
+        w1_sc = [[held("w1_sc%d%d" % (b, a), [P, KP], U8) for a in range(NPASS)] for b in range(NBLK)]
+        seen_sb = [held("seen%d" % b, [P, PACK, S], F32) for b in range(NBLK)]
+        v = [held("v%d" % a, [P, S], U32) for a in range(NPASS)]
+        v_sc = [held("v_sc%d" % a, [P, S], U8) for a in range(NPASS)]
+        v2 = [held("v2_%d" % a, [P, S2], U32) for a in range(NPASS)]
+        v2_sc = held("v2_sc", [P, S2], U8)
+        larger = [held("larger%d" % b, [P, PACK, S], F32) for b in range(NBLK)]
+        h_bf = [held("h_bf%d" % b, [P, S * PACK], BF16) for b in range(NBLK)]
+        h_q = [held("h_q%d" % b, [P, S], U32) for b in range(NBLK)]
+        h_sc = [held("h_sc%d" % b, [P, S], U8) for b in range(NBLK)]
+        ba_sb = held("ba_sb", [P, MT], F32)
+        bt_sb = held("bt_sb", [P, MT], F32)
+        wgo_sb = held("wgo_sb", [P, S], F32)
+        page = [held("page%d" % q, [P, T2], F32) for q in range(MT)]
+        gate = [held("gate%d" % q, [P, S], F32) for q in range(MT)]
+        gate_w = [held("gate_w%d" % q, [P, S], F32) for q in range(MT)]
+        score = [held("score%d" % q, [P, S], F32) for q in range(MT)]
+
+        def load_words(dst, words, a):
+            nc.sync.dma_start(dst[a][:], words[a].rearrange("p t i -> p (t i)").bitcast(I32))
+
+        def load_w1(b, a):
+            nc.sync.dma_start(w1_raw[b][a][:],
+                              w1[a * KP:(a + 1) * KP, b * KP:(b + 1) * KP].rearrange("(p i) c -> p i c", i=PACK))
+
+        def load_seen(b):
+            nc.sync.dma_start(seen_sb[b][:], seen[b * KP:(b + 1) * KP, :].rearrange("(p t) j -> p t j", t=PACK))
+
+        def load_planes_side_by_side(queue, dst, scales):
+            for quad in range(4):
+                queue.dma_start(dst[32 * quad:32 * quad + 4, :].bitcast(I32).rearrange("r (a n) -> r a n", a=NPASS),
+                                scales[:, 4 * quad:4 * quad + 4, :].bitcast(I32).rearrange("a r n -> r a n"))
+
+        def cast_w1(b, a):
+            nc.scalar.copy(w1_bf[b][a][:].rearrange("p (t m i) -> p m i t", t=PACK, i=PACK),
+                           w1_raw[b][a][:].rearrange("p i (m t) -> p m i t", t=PACK))
+
+        def quantize(codes, scales, values):
+            nc.vector.quantize_mx(out=codes[:].bitcast(FP8X4), scales=scales[:], in_=values[:])
+
+        def gather_words(dst, src, offsets):
+            nc.vector.tensor_copy(dst[:], src[:].bitcast(U32).indirect(offsets[:]))
+
+        def w1_pass(banks, b, a):
+            for t in range(PACK):
+                cols = slice(t * P, (t + 1) * P)
+                nc.tensor.matmul_mx(out=banks[t][:], lhsT=w1_q[b][a][:, cols].bitcast(FP8X4), lhsT_scale=w1_sc[b][a][:, cols],
+                                    rhs=v[a][:].bitcast(FP8X4), rhs_scale=v_sc[a][:], start=(a == 0), stop=(a == NPASS - 1))
+
+        def w4_pass(banks, b, a):
+            for jq in range(JQ):
+                jams = slice(jq * P, (jq + 1) * P)
+                for t in range(PACK):
+                    c0 = a * H + b * KP + t * P
+                    nc.tensor.matmul_mx(out=banks[jq][:, t * P:(t + 1) * P], lhsT=w4[:, 2 * c0:2 * (c0 + P)].bitcast(FP4X4),
+                                        lhsT_scale=w4_sc[:, c0:c0 + P], rhs=v[a][:, jams].bitcast(FP8X4),
+                                        rhs_scale=v_sc[a][:, jams], start=(a == 0 and t == 0),
+                                        stop=(a == NPASS - 1 and t == PACK - 1))
+
+        def take_larger(banks, b):
+            for t in range(PACK):
+                nc.vector.tensor_tensor(larger[b][:, t, :], banks[t][:], seen_sb[b][:, t, :], ALU.max)
+
+        def add_w4(banks, b):
+            for jq in range(JQ):
+                nc.vector.tensor_tensor(
+                    h_bf[b][:, jq * KP:(jq + 1) * KP].rearrange("p (c i t) -> p c t i", i=4, t=PACK),
+                    banks[jq][:].rearrange("p (t c i) -> p c t i", t=PACK, i=4),
+                    larger[b][:, :, jq * P:(jq + 1) * P].rearrange("p t (c i) -> p c t i", i=4), ALU.add)
+
+        def lineup_product(bank, q, codes, scales):
+            cols = slice(q * P, (q + 1) * P)
+            for a in range(NPASS):
+                nc.tensor.matmul_mx(out=bank[:], lhsT=v2[a][:, cols].bitcast(FP8X4), lhsT_scale=v2_sc[4 * a:P, cols],
+                                    rhs=codes[a][:].bitcast(FP8X4), rhs_scale=scales[a][:], start=(a == 0), stop=(a == NPASS - 1))
+
+        def banks_of(tag):
+            return [psum.tile([P, S], F32, name=tag, tag=tag) for n in range(4)]
+
+        nc.vector.memset(w4_sc_raw[:].bitcast(I32), 0)
+        nc.vector.memset(tab_sc[:].bitcast(I32), 0)
+        nc.gpsimd.memset(tab2_sc[:].bitcast(I32), 0)
+
+        nc.sync.dma_start(idx[:], offs)
+        nc.sync.dma_start(w4_raw[:].bitcast(I32).rearrange("p (a n) -> p a n", a=NPASS),
+                          w4_words.bitcast(I32).rearrange("a p n -> p a n"))
+        load_w1(0, 0)
+        load_planes_side_by_side(nc.scalar, w4_sc_raw, w4_scales)
+        load_planes_side_by_side(nc.scalar, tab_sc, tab_scales)
+        for quad in range(4):
+            nc.gpsimd.dma_start(tab2_sc[32 * quad:32 * quad + 4 * NPASS, :].bitcast(I32),
+                                tab2_scales[:, 4 * quad:4 * quad + 4, :].bitcast(I32))
+        load_words(tab, tab_words, 0)
+        load_w1(0, 1)
+        load_words(tab, tab_words, 1)
+        nc.sync.dma_start(idx2[:], offs2)
+        load_seen(0)
+        load_w1(1, 0)
+        load_words(tab2, tab2_words, 0)
+        load_w1(1, 1)
+        load_seen(1)
+        load_words(tab2, tab2_words, 1)
+        with nc.allow_non_contiguous_dma(reason="one bias value a partition"):
+            nc.sync.dma_start(bt_sb[:], bt.rearrange("(q p) -> p q", p=P))
+            nc.sync.dma_start(ba_sb[:], ba.rearrange("(q p) -> p q", p=P))
+        nc.sync.dma_start(wgo_sb[:], wgo)
+        nc.sync.dma_start(idx3[:], offs3)
+        for q in range(MT):
+            nc.sync.dma_start(page[q][:], page1[q * P:(q + 1) * P, :])
+
+        nc.vector.tensor_copy(w4[:].bitcast(U16).rearrange("p (g t m) -> p g t m", t=PACK, m=P),
+                              w4_raw[:].bitcast(U16).rearrange("p (g m t) -> p g t m", t=PACK, m=P))
+        nc.vector.tensor_copy(w4_sc[:].rearrange("p (g t m) -> p g t m", t=PACK, m=P),
+                              w4_sc_raw[:].rearrange("p (g m t) -> p g t m", t=PACK, m=P))
+        for a in range(NPASS):
+            nc.vector.tensor_copy(v_sc[a][:], tab_sc[:, a * T:(a + 1) * T].indirect(idx[:]))
+
+        cast_w1(0, 0)
+        cast_w1(0, 1)
+        quantize(w1_q[0][0], w1_sc[0][0], w1_bf[0][0])
+        gather_words(v[0], tab[0], idx)
+        nc.vector.tensor_copy(v2_sc[:], tab2_sc[:].indirect(idx2[:]))
+        gather_words(v[1], tab[1], idx)
+        quantize(w1_q[0][1], w1_sc[0][1], w1_bf[0][1])
+        first, second = banks_of("first"), banks_of("second")
+        w1_pass(first, 0, 0)
+        w4_pass(second, 0, 0)
+        w1_pass(first, 0, 1)
+        w4_pass(second, 0, 1)
+        take_larger(first, 0)
+        add_w4(second, 0)
+
+        cast_w1(1, 0)
+        cast_w1(1, 1)
+        quantize(w1_q[1][0], w1_sc[1][0], w1_bf[1][0])
+        quantize(h_q[0], h_sc[0], h_bf[0])
+        gather_words(v2[0], tab2[0], idx2)
+        quantize(w1_q[1][1], w1_sc[1][1], w1_bf[1][1])
+        first, second = banks_of("first"), banks_of("second")
+        w1_pass(first, 1, 0)
+        w4_pass(second, 1, 0)
+        w4_pass(second, 1, 1)
+        w1_pass(first, 1, 1)
+        take_larger(first, 1)
+        gather_words(v2[1], tab2[1], idx2)
+        add_w4(second, 1)
+        quantize(h_q[1], h_sc[1], h_bf[1])
+
+        first, second = banks_of("first"), banks_of("second")
+        for q in range(MT):
+            lineup_product(first[q], q, v, v_sc)
+            nc.scalar.activation(gate[q][:], first[q][:], ACT.Tanh, bias=bt_sb[:, q:q + 1])
+        for q in range(MT):
+            lineup_product(second[q], q, h_q, h_sc)
+            nc.scalar.activation(score[q][:], second[q][:], ACT.Identity, bias=ba_sb[:, q:q + 1])
+        for q in range(MT):
+            nc.vector.tensor_tensor(gate_w[q][:], gate[q][:], wgo_sb[:], ALU.mult)
+        for q in range(MT):
+            nc.vector.tensor_tensor(page[q][:].indirect(idx3[:]), score[q][:], gate_w[q][:], ALU.mult)
+            nc.sync.dma_start(out[q * P:(q + 1) * P, :], page[q][:])

@@ -1,6 +1,7 @@
 from contextlib import ExitStack
 
 import concourse.mybir as mybir
+from concourse.masks import make_identity
 
 K, H, T, S, T3, S2, T2 = 1024, 1024, 2048, 512, 2048, 512, 1024
 FLOPS = 2 * (2 * K * H * S + 2 * H * S2 * S)
@@ -46,11 +47,13 @@ def tile_list_derby_jam_lineups_kernel(tc, tab_words, tab_scales, offs, tab2_wor
         w4_sc_raw = held("w4_sc_raw", [P, NPASS * H], U8)
         w4 = held("w4", [P, NPASS * 2 * H], U8)
         w4_sc = held("w4_sc", [P, NPASS * H], U8)
-        w1_raw = [[held("w1_raw%d%d" % (b, a), [P, PACK, KP], F32) for a in range(NPASS)] for b in range(NBLK)]
+        pieces = [[1, 1], [1, 2]]
+        w1_raw = [[[held("w1_raw%d%d%d" % (b, a, u), [P, PACK, KP // pieces[b][a]], F32) for u in range(pieces[b][a])]
+                   for a in range(NPASS)] for b in range(NBLK)]
         w1_bf = [[held("w1_bf%d%d" % (b, a), [P, KP * PACK], BF16) for a in range(NPASS)] for b in range(NBLK)]
         w1_q = [[held("w1_q%d%d" % (b, a), [P, KP], U32) for a in range(NPASS)] for b in range(NBLK)]
         w1_sc = [[held("w1_sc%d%d" % (b, a), [P, KP], U8) for a in range(NPASS)] for b in range(NBLK)]
-        seen_sb = [held("seen%d" % b, [P, PACK, S], F32) for b in range(NBLK)]
+        seen_sb = [[held("seen%d%d" % (b, u), [P, 2, S], F32) for u in range(2)] for b in range(NBLK)]
         v = [held("v%d" % a, [P, S], U32) for a in range(NPASS)]
         v_sc = [held("v_sc%d" % a, [P, S], U8) for a in range(NPASS)]
         v2 = [held("v2_%d" % a, [P, S2], U32) for a in range(NPASS)]
@@ -59,8 +62,9 @@ def tile_list_derby_jam_lineups_kernel(tc, tab_words, tab_scales, offs, tab2_wor
         h_bf = [held("h_bf%d" % b, [P, S * PACK], BF16) for b in range(NBLK)]
         h_q = [held("h_q%d" % b, [P, S], U32) for b in range(NBLK)]
         h_sc = [held("h_sc%d" % b, [P, S], U8) for b in range(NBLK)]
-        ba_sb = held("ba_sb", [P, MT], F32)
-        bt_sb = held("bt_sb", [P, MT], F32)
+        bias_rows = held("bias_rows", [P, P], F32)
+        identity = held("identity", [P, P], F32)
+        bias = held("bias", [P, 2 * MT], F32)
         wgo_sb = held("wgo_sb", [P, S], F32)
         page = [held("page%d" % q, [P, T2], F32) for q in range(MT)]
         gate = [held("gate%d" % q, [P, S], F32) for q in range(MT)]
@@ -71,11 +75,16 @@ def tile_list_derby_jam_lineups_kernel(tc, tab_words, tab_scales, offs, tab2_wor
             nc.sync.dma_start(dst[a][:], words[a].rearrange("p t i -> p (t i)").bitcast(I32))
 
         def load_w1(b, a):
-            nc.sync.dma_start(w1_raw[b][a][:],
-                              w1[a * KP:(a + 1) * KP, b * KP:(b + 1) * KP].rearrange("(p i) c -> p i c", i=PACK))
+            width = KP // pieces[b][a]
+            for u in range(pieces[b][a]):
+                c0 = b * KP + u * width
+                nc.sync.dma_start(w1_raw[b][a][u][:],
+                                  w1[a * KP:(a + 1) * KP, c0:c0 + width].rearrange("(p i) c -> p i c", i=PACK))
 
         def load_seen(b):
-            nc.sync.dma_start(seen_sb[b][:], seen[b * KP:(b + 1) * KP, :].rearrange("(p t) j -> p t j", t=PACK))
+            rows = seen[b * KP:(b + 1) * KP, :].rearrange("(p t) j -> p t j", t=PACK)
+            for u in range(2):
+                nc.sync.dma_start(seen_sb[b][u][:], rows[:, 2 * u:2 * u + 2, :])
 
         def load_planes_side_by_side(queue, dst, scales):
             for quad in range(4):
@@ -83,11 +92,13 @@ def tile_list_derby_jam_lineups_kernel(tc, tab_words, tab_scales, offs, tab2_wor
                                 scales[:, 4 * quad:4 * quad + 4, :].bitcast(I32).rearrange("a r n -> r a n"))
 
         def cast_w1(b, a):
-            nc.scalar.copy(w1_bf[b][a][:].rearrange("p (t m i) -> p m i t", t=PACK, i=PACK),
-                           w1_raw[b][a][:].rearrange("p i (m t) -> p m i t", t=PACK))
+            width = P // pieces[b][a]
+            dealt = w1_bf[b][a][:].rearrange("p (t m i) -> p m i t", t=PACK, i=PACK)
+            for u in range(pieces[b][a]):
+                nc.scalar.copy(dealt[:, u * width:(u + 1) * width], w1_raw[b][a][u][:].rearrange("p i (m t) -> p m i t", t=PACK))
 
         def quantize(codes, scales, values):
-            nc.vector.quantize_mx(out=codes[:].bitcast(FP8X4), scales=scales[:], in_=values[:])
+            nc.vector.quantize_mx(out=codes.bitcast(FP8X4), scales=scales, in_=values)
 
         def gather_words(dst, src, offsets):
             nc.vector.tensor_copy(dst[:], src[:].bitcast(U32).indirect(offsets[:]))
@@ -110,100 +121,103 @@ def tile_list_derby_jam_lineups_kernel(tc, tab_words, tab_scales, offs, tab2_wor
 
         def take_larger(banks, b):
             for t in range(PACK):
-                nc.vector.tensor_tensor(larger[b][:, t, :], banks[t][:], seen_sb[b][:, t, :], ALU.max)
+                nc.vector.tensor_tensor(larger[b][:, t, :], banks[t][:], seen_sb[b][t // 2][:, t % 2, :], ALU.max)
 
-        def add_w4(banks, b):
-            for jq in range(JQ):
+        def add_w4(banks, b, quarters):
+            for jq in quarters:
                 nc.vector.tensor_tensor(
                     h_bf[b][:, jq * KP:(jq + 1) * KP].rearrange("p (c i t) -> p c t i", i=4, t=PACK),
                     banks[jq][:].rearrange("p (t c i) -> p c t i", t=PACK, i=4),
                     larger[b][:, :, jq * P:(jq + 1) * P].rearrange("p t (c i) -> p c t i", i=4), ALU.add)
 
-        def lineup_product(bank, q, codes, scales):
+        def lineup_product(bank, q, codes, scales, jams):
             cols = slice(q * P, (q + 1) * P)
             for a in range(NPASS):
-                nc.tensor.matmul_mx(out=bank[:], lhsT=v2[a][:, cols].bitcast(FP8X4), lhsT_scale=v2_sc[4 * a:P, cols],
-                                    rhs=codes[a][:].bitcast(FP8X4), rhs_scale=scales[a][:], start=(a == 0), stop=(a == NPASS - 1))
+                nc.tensor.matmul_mx(out=bank, lhsT=v2[a][:, cols].bitcast(FP8X4), lhsT_scale=v2_sc[8 + 4 * a:P, cols],
+                                    rhs=codes[a][:, jams].bitcast(FP8X4), rhs_scale=scales[a][:, jams], start=(a == 0), stop=(a == NPASS - 1))
 
         def banks_of(tag):
             return [psum.tile([P, S], F32, name=tag, tag=tag) for n in range(4)]
 
-        nc.vector.memset(w4_sc_raw[:].bitcast(I32), 0)
+        nc.gpsimd.memset(w4_sc_raw[:].bitcast(I32), 0)
         nc.vector.memset(tab_sc[:].bitcast(I32), 0)
         nc.gpsimd.memset(tab2_sc[:].bitcast(I32), 0)
+        nc.gpsimd.memset(bias_rows[:], 0.0)
 
         nc.sync.dma_start(idx[:], offs)
         nc.sync.dma_start(w4_raw[:].bitcast(I32).rearrange("p (a n) -> p a n", a=NPASS),
                           w4_words.bitcast(I32).rearrange("a p n -> p a n"))
         load_w1(0, 0)
-        load_planes_side_by_side(nc.scalar, w4_sc_raw, w4_scales)
-        load_planes_side_by_side(nc.scalar, tab_sc, tab_scales)
+        nc.sync.dma_start(idx3[:], offs3)
+        load_planes_side_by_side(nc.sync, w4_sc_raw, w4_scales)
         for quad in range(4):
-            nc.gpsimd.dma_start(tab2_sc[32 * quad:32 * quad + 4 * NPASS, :].bitcast(I32),
+            nc.gpsimd.dma_start(tab2_sc[32 * quad + 8:32 * quad + 16, :].bitcast(I32),
                                 tab2_scales[:, 4 * quad:4 * quad + 4, :].bitcast(I32))
         load_words(tab, tab_words, 0)
+        load_planes_side_by_side(nc.sync, tab_sc, tab_scales)
         load_w1(0, 1)
         load_words(tab, tab_words, 1)
-        nc.sync.dma_start(idx2[:], offs2)
         load_seen(0)
+        nc.sync.dma_start(idx2[:], offs2)
+        nc.sync.dma_start(bias_rows[0:MT, :], bt.rearrange("(q p) -> q p", p=P))
+        nc.sync.dma_start(bias_rows[MT:2 * MT, :], ba.rearrange("(q p) -> q p", p=P))
         load_w1(1, 0)
         load_words(tab2, tab2_words, 0)
         load_w1(1, 1)
         load_seen(1)
         load_words(tab2, tab2_words, 1)
-        with nc.allow_non_contiguous_dma(reason="one bias value a partition"):
-            nc.sync.dma_start(bt_sb[:], bt.rearrange("(q p) -> p q", p=P))
-            nc.sync.dma_start(ba_sb[:], ba.rearrange("(q p) -> p q", p=P))
         nc.sync.dma_start(wgo_sb[:], wgo)
-        nc.sync.dma_start(idx3[:], offs3)
         for q in range(MT):
             nc.sync.dma_start(page[q][:], page1[q * P:(q + 1) * P, :])
+        make_identity(nc, identity[:])
 
         nc.vector.tensor_copy(w4[:].bitcast(U16).rearrange("p (g t m) -> p g t m", t=PACK, m=P),
                               w4_raw[:].bitcast(U16).rearrange("p (g m t) -> p g t m", t=PACK, m=P))
         nc.vector.tensor_copy(w4_sc[:].rearrange("p (g t m) -> p g t m", t=PACK, m=P),
                               w4_sc_raw[:].rearrange("p (g m t) -> p g t m", t=PACK, m=P))
-        for a in range(NPASS):
-            nc.vector.tensor_copy(v_sc[a][:], tab_sc[:, a * T:(a + 1) * T].indirect(idx[:]))
-
         cast_w1(0, 0)
         cast_w1(0, 1)
-        quantize(w1_q[0][0], w1_sc[0][0], w1_bf[0][0])
+        quantize(w1_q[0][0][:], w1_sc[0][0][:], w1_bf[0][0][:])
         gather_words(v[0], tab[0], idx)
-        nc.vector.tensor_copy(v2_sc[:], tab2_sc[:].indirect(idx2[:]))
+        for a in range(NPASS):
+            nc.vector.tensor_copy(v_sc[a][:], tab_sc[:, a * T:(a + 1) * T].indirect(idx[:]))
+        quantize(w1_q[0][1][:], w1_sc[0][1][:], w1_bf[0][1][:])
         gather_words(v[1], tab[1], idx)
-        quantize(w1_q[0][1], w1_sc[0][1], w1_bf[0][1])
         first, second = banks_of("first"), banks_of("second")
         w1_pass(first, 0, 0)
         w4_pass(second, 0, 0)
         w1_pass(first, 0, 1)
         w4_pass(second, 0, 1)
+        nc.vector.tensor_copy(v2_sc[:], tab2_sc[:].indirect(idx2[:]))
         take_larger(first, 0)
-        add_w4(second, 0)
+        add_w4(second, 0, range(JQ))
 
+        turned = psum.tile([P, S], F32, name="second", tag="second")
+        nc.tensor.transpose(turned[:, 0:P], bias_rows[:], identity[:])
         cast_w1(1, 0)
+        nc.scalar.copy(bias[:], turned[:, 0:2 * MT])
         cast_w1(1, 1)
-        quantize(w1_q[1][0], w1_sc[1][0], w1_bf[1][0])
-        quantize(h_q[0], h_sc[0], h_bf[0])
+        quantize(w1_q[1][0][:], w1_sc[1][0][:], w1_bf[1][0][:])
         gather_words(v2[0], tab2[0], idx2)
-        quantize(w1_q[1][1], w1_sc[1][1], w1_bf[1][1])
+        quantize(w1_q[1][1][:], w1_sc[1][1][:], w1_bf[1][1][:])
+        quantize(h_q[0][:], h_sc[0][:], h_bf[0][:])
         first, second = banks_of("first"), banks_of("second")
-        w1_pass(first, 1, 0)
         w4_pass(second, 1, 0)
+        w1_pass(first, 1, 0)
         w4_pass(second, 1, 1)
         w1_pass(first, 1, 1)
         take_larger(first, 1)
         gather_words(v2[1], tab2[1], idx2)
-        add_w4(second, 1)
-        quantize(h_q[1], h_sc[1], h_bf[1])
+        add_w4(second, 1, range(JQ))
+        quantize(h_q[1][:], h_sc[1][:], h_bf[1][:])
 
         first, second = banks_of("first"), banks_of("second")
         for q in range(MT):
-            lineup_product(first[q], q, v, v_sc)
-            nc.scalar.activation(gate[q][:], first[q][:], ACT.Tanh, bias=bt_sb[:, q:q + 1])
+            lineup_product(first[q][:], q, v, v_sc, slice(0, S))
+            nc.scalar.activation(gate[q][:], first[q][:], ACT.Tanh, bias=bias[:, q:q + 1])
         for q in range(MT):
-            lineup_product(second[q], q, h_q, h_sc)
-            nc.scalar.activation(score[q][:], second[q][:], ACT.Identity, bias=ba_sb[:, q:q + 1])
+            lineup_product(second[q][:], q, h_q, h_sc, slice(0, S))
+            nc.scalar.activation(score[q][:], second[q][:], ACT.Identity, bias=bias[:, MT + q:MT + q + 1])
         for q in range(MT):
             nc.vector.tensor_tensor(gate_w[q][:], gate[q][:], wgo_sb[:], ALU.mult)
         for q in range(MT):

@@ -24,6 +24,7 @@ NPASS = K // KP
 NBLK = H // KP
 MT = S2 // P
 JQ = S // P
+HALF = S // 2
 
 
 def tile_list_derby_jam_lineups_kernel(tc, tab_words, tab_scales, offs, tab2_words, tab2_scales, offs2, offs3,
@@ -58,7 +59,7 @@ def tile_list_derby_jam_lineups_kernel(tc, tab_words, tab_scales, offs, tab2_wor
         v_sc = [held("v_sc%d" % a, [P, S], U8) for a in range(NPASS)]
         v2 = [held("v2_%d" % a, [P, S2], U32) for a in range(NPASS)]
         v2_sc = held("v2_sc", [P, S2], U8)
-        larger = [held("larger%d" % b, [P, PACK, S], F32) for b in range(NBLK)]
+        larger = [held("larger%d" % b, [P, 2, S, 2], F32) for b in range(NBLK)]
         h_bf = [held("h_bf%d" % b, [P, S * PACK], BF16) for b in range(NBLK)]
         h_q = [held("h_q%d" % b, [P, S], U32) for b in range(NBLK)]
         h_sc = [held("h_sc%d" % b, [P, S], U8) for b in range(NBLK)]
@@ -93,9 +94,10 @@ def tile_list_derby_jam_lineups_kernel(tc, tab_words, tab_scales, offs, tab2_wor
 
         def cast_w1(b, a):
             width = P // pieces[b][a]
-            dealt = w1_bf[b][a][:].rearrange("p (t m i) -> p m i t", t=PACK, i=PACK)
+            dealt = w1_bf[b][a][:].rearrange("p (t m x y) -> p m x t y", t=PACK, x=2, y=2)
             for u in range(pieces[b][a]):
-                nc.scalar.copy(dealt[:, u * width:(u + 1) * width], w1_raw[b][a][u][:].rearrange("p i (m t) -> p m i t", t=PACK))
+                nc.scalar.copy(dealt[:, u * width:(u + 1) * width],
+                               w1_raw[b][a][u][:].rearrange("p (x y) (m t) -> p m x t y", y=2, t=PACK))
 
         def quantize(codes, scales, values):
             nc.vector.quantize_mx(out=codes.bitcast(FP8X4), scales=scales, in_=values)
@@ -104,10 +106,15 @@ def tile_list_derby_jam_lineups_kernel(tc, tab_words, tab_scales, offs, tab2_wor
             nc.vector.tensor_copy(dst[:], src[:].bitcast(U32).indirect(offsets[:]))
 
         def w1_pass(banks, b, a):
-            for t in range(PACK):
-                cols = slice(t * P, (t + 1) * P)
-                nc.tensor.matmul_mx(out=banks[t][:], lhsT=w1_q[b][a][:, cols].bitcast(FP8X4), lhsT_scale=w1_sc[b][a][:, cols],
-                                    rhs=v[a][:].bitcast(FP8X4), rhs_scale=v_sc[a][:], start=(a == 0), stop=(a == NPASS - 1))
+            for x in range(2):
+                for u in range(2):
+                    jams = slice(u * HALF, (u + 1) * HALF)
+                    for y in range(2):
+                        cols = slice((2 * x + y) * P, (2 * x + y + 1) * P)
+                        nc.tensor.matmul_mx(out=banks[2 * x + u][:, y * HALF:(y + 1) * HALF], lhsT=w1_q[b][a][:, cols].bitcast(FP8X4),
+                                            lhsT_scale=w1_sc[b][a][:, cols], rhs=v[a][:, jams].bitcast(FP8X4),
+                                            rhs_scale=v_sc[a][:, jams], start=(a == 0 and y == 0),
+                                            stop=(a == NPASS - 1 and y == 1))
 
         def w4_pass(banks, b, a):
             for jq in range(JQ):
@@ -120,15 +127,18 @@ def tile_list_derby_jam_lineups_kernel(tc, tab_words, tab_scales, offs, tab2_wor
                                         stop=(a == NPASS - 1 and t == PACK - 1))
 
         def take_larger(banks, b):
-            for t in range(PACK):
-                nc.vector.tensor_tensor(larger[b][:, t, :], banks[t][:], seen_sb[b][t // 2][:, t % 2, :], ALU.max)
+            for x in range(2):
+                for u in range(2):
+                    jams = slice(u * HALF, (u + 1) * HALF)
+                    nc.vector.tensor_tensor(larger[b][:, x, jams, :], banks[2 * x + u][:].rearrange("p (y j) -> p j y", y=2),
+                                            seen_sb[b][x][:, :, jams].rearrange("p y j -> p j y"), ALU.max)
 
         def add_w4(banks, b, quarters):
             for jq in quarters:
                 nc.vector.tensor_tensor(
-                    h_bf[b][:, jq * KP:(jq + 1) * KP].rearrange("p (c i t) -> p c t i", i=4, t=PACK),
-                    banks[jq][:].rearrange("p (t c i) -> p c t i", t=PACK, i=4),
-                    larger[b][:, :, jq * P:(jq + 1) * P].rearrange("p t (c i) -> p c t i", i=4), ALU.add)
+                    h_bf[b][:, jq * KP:(jq + 1) * KP].rearrange("p (j x y) -> p j x y", x=2, y=2),
+                    banks[jq][:].rearrange("p (x y j) -> p j x y", x=2, y=2),
+                    larger[b][:, :, jq * P:(jq + 1) * P, :].rearrange("p x j y -> p j x y"), ALU.add)
 
         def lineup_product(bank, q, codes, scales, jams):
             cols = slice(q * P, (q + 1) * P)
@@ -157,8 +167,8 @@ def tile_list_derby_jam_lineups_kernel(tc, tab_words, tab_scales, offs, tab2_wor
         load_planes_side_by_side(nc.sync, tab_sc, tab_scales)
         load_w1(0, 1)
         load_words(tab, tab_words, 1)
-        load_seen(0)
         nc.sync.dma_start(idx2[:], offs2)
+        load_seen(0)
         nc.sync.dma_start(bias_rows[0:MT, :], bt.rearrange("(q p) -> q p", p=P))
         nc.sync.dma_start(bias_rows[MT:2 * MT, :], ba.rearrange("(q p) -> q p", p=P))
         load_w1(1, 0)
@@ -202,10 +212,10 @@ def tile_list_derby_jam_lineups_kernel(tc, tab_words, tab_scales, offs, tab2_wor
         quantize(w1_q[1][1][:], w1_sc[1][1][:], w1_bf[1][1][:])
         quantize(h_q[0][:], h_sc[0][:], h_bf[0][:])
         first, second = banks_of("first"), banks_of("second")
-        w4_pass(second, 1, 0)
         w1_pass(first, 1, 0)
-        w4_pass(second, 1, 1)
         w1_pass(first, 1, 1)
+        w4_pass(second, 1, 0)
+        w4_pass(second, 1, 1)
         take_larger(first, 1)
         gather_words(v2[1], tab2[1], idx2)
         add_w4(second, 1, range(JQ))

@@ -32,7 +32,7 @@ def tile_list_derby_jam_lineups_kernel(tc, tab_words, tab_scales, offs, tab2_wor
     nc = tc.nc
     with ExitStack() as ctx:
         keep = ctx.enter_context(tc.tile_pool(name="keep", bufs=1))
-        psum = ctx.enter_context(tc.psum_pool(name="psum", bufs=4))
+        psum = ctx.enter_context(tc.psum_pool(name="psum", bufs=1))
 
         def held(name, shape, dtype):
             return keep.tile(shape, dtype, name=name, align_bytes=64)
@@ -82,10 +82,9 @@ def tile_list_derby_jam_lineups_kernel(tc, tab_words, tab_scales, offs, tab2_wor
                 nc.sync.dma_start(w1_raw[b][a][u][:],
                                   w1[a * KP:(a + 1) * KP, c0:c0 + width].rearrange("(p i) c -> p i c", i=PACK))
 
-        def load_seen(b):
+        def load_seen(b, x):
             rows = seen[b * KP:(b + 1) * KP, :].rearrange("(p t) j -> p t j", t=PACK)
-            for u in range(2):
-                nc.sync.dma_start(seen_sb[b][u][:], rows[:, 2 * u:2 * u + 2, :])
+            nc.sync.dma_start(seen_sb[b][x][:], rows[:, 2 * x:2 * x + 2, :])
 
         def load_planes_side_by_side(queue, dst, scales):
             for quad in range(4):
@@ -116,8 +115,8 @@ def tile_list_derby_jam_lineups_kernel(tc, tab_words, tab_scales, offs, tab2_wor
                                             rhs_scale=v_sc[a][:, jams], start=(a == 0 and y == 0),
                                             stop=(a == NPASS - 1 and y == 1))
 
-        def w4_pass(banks, b, a):
-            for jq in range(JQ):
+        def w4_pass(banks, b, a, quarters):
+            for jq in quarters:
                 jams = slice(jq * P, (jq + 1) * P)
                 for t in range(PACK):
                     c0 = a * H + b * KP + t * P
@@ -146,37 +145,39 @@ def tile_list_derby_jam_lineups_kernel(tc, tab_words, tab_scales, offs, tab2_wor
                 nc.tensor.matmul_mx(out=bank, lhsT=v2[a][:, cols].bitcast(FP8X4), lhsT_scale=v2_sc[8 + 4 * a:P, cols],
                                     rhs=codes[a][:, jams].bitcast(FP8X4), rhs_scale=scales[a][:, jams], start=(a == 0), stop=(a == NPASS - 1))
 
-        def banks_of(tag):
-            return [psum.tile([P, S], F32, name=tag, tag=tag) for n in range(4)]
+        def banks_at(*numbers):
+            return [psum.tile([P, S], F32, name="bank%d" % n, tag="bank%d" % n) for n in numbers]
 
         nc.gpsimd.memset(w4_sc_raw[:].bitcast(I32), 0)
         nc.vector.memset(tab_sc[:].bitcast(I32), 0)
         nc.gpsimd.memset(tab2_sc[:].bitcast(I32), 0)
         nc.gpsimd.memset(bias_rows[:], 0.0)
 
-        nc.sync.dma_start(idx[:], offs)
         nc.sync.dma_start(w4_raw[:].bitcast(I32).rearrange("p (a n) -> p a n", a=NPASS),
                           w4_words.bitcast(I32).rearrange("a p n -> p a n"))
-        load_w1(0, 0)
+        nc.sync.dma_start(idx[:], offs)
         nc.sync.dma_start(idx3[:], offs3)
         load_planes_side_by_side(nc.sync, w4_sc_raw, w4_scales)
-        for quad in range(4):
-            nc.gpsimd.dma_start(tab2_sc[32 * quad + 8:32 * quad + 16, :].bitcast(I32),
-                                tab2_scales[:, 4 * quad:4 * quad + 4, :].bitcast(I32))
-        load_words(tab, tab_words, 0)
+        load_w1(0, 0)
+        nc.gpsimd.dma_start(bias_rows[0:MT, :], bt.rearrange("(q p) -> q p", p=P))
+        nc.gpsimd.dma_start(bias_rows[MT:2 * MT, :], ba.rearrange("(q p) -> q p", p=P))
         load_planes_side_by_side(nc.sync, tab_sc, tab_scales)
+        load_words(tab, tab_words, 0)
         load_w1(0, 1)
-        load_words(tab, tab_words, 1)
+        for quad in range(4):
+            nc.sync.dma_start(tab2_sc[32 * quad + 8:32 * quad + 16, :].bitcast(I32),
+                              tab2_scales[:, 4 * quad:4 * quad + 4, :].bitcast(I32))
         nc.sync.dma_start(idx2[:], offs2)
-        load_seen(0)
-        nc.sync.dma_start(bias_rows[0:MT, :], bt.rearrange("(q p) -> q p", p=P))
-        nc.sync.dma_start(bias_rows[MT:2 * MT, :], ba.rearrange("(q p) -> q p", p=P))
+        load_words(tab, tab_words, 1)
+        load_seen(0, 0)
+        load_seen(0, 1)
         load_w1(1, 0)
         load_words(tab2, tab2_words, 0)
         load_w1(1, 1)
-        load_seen(1)
         load_words(tab2, tab2_words, 1)
+        load_seen(1, 0)
         nc.sync.dma_start(wgo_sb[:], wgo)
+        load_seen(1, 1)
         for q in range(MT):
             nc.sync.dma_start(page[q][:], page1[q * P:(q + 1) * P, :])
         make_identity(nc, identity[:])
@@ -185,24 +186,26 @@ def tile_list_derby_jam_lineups_kernel(tc, tab_words, tab_scales, offs, tab2_wor
                               w4_raw[:].bitcast(U16).rearrange("p (g m t) -> p g t m", t=PACK, m=P))
         nc.vector.tensor_copy(w4_sc[:].rearrange("p (g t m) -> p g t m", t=PACK, m=P),
                               w4_sc_raw[:].rearrange("p (g m t) -> p g t m", t=PACK, m=P))
-        cast_w1(0, 0)
-        cast_w1(0, 1)
-        quantize(w1_q[0][0][:], w1_sc[0][0][:], w1_bf[0][0][:])
-        gather_words(v[0], tab[0], idx)
         for a in range(NPASS):
             nc.vector.tensor_copy(v_sc[a][:], tab_sc[:, a * T:(a + 1) * T].indirect(idx[:]))
-        quantize(w1_q[0][1][:], w1_sc[0][1][:], w1_bf[0][1][:])
-        gather_words(v[1], tab[1], idx)
-        first, second = banks_of("first"), banks_of("second")
-        w1_pass(first, 0, 0)
-        w4_pass(second, 0, 0)
-        w1_pass(first, 0, 1)
-        w4_pass(second, 0, 1)
+        cast_w1(0, 0)
+        cast_w1(0, 1)
+        gather_words(v[0], tab[0], idx)
+        quantize(w1_q[0][0][:], w1_sc[0][0][:], w1_bf[0][0][:])
         nc.vector.tensor_copy(v2_sc[:], tab2_sc[:].indirect(idx2[:]))
+        quantize(w1_q[0][1][:], w1_sc[0][1][:], w1_bf[0][1][:])
+        for u in range(2):
+            nc.vector.tensor_copy(v[1][:, u * HALF:(u + 1) * HALF],
+                                  tab[1][:].bitcast(U32).indirect(idx[:, u * HALF // 16:(u + 1) * HALF // 16]))
+        first, second = banks_at(0, 1, 2, 3), banks_at(4, 5, 6, 7)
+        w1_pass(first, 0, 0)
+        w4_pass(second, 0, 0, range(JQ))
+        w1_pass(first, 0, 1)
+        w4_pass(second, 0, 1, range(JQ))
         take_larger(first, 0)
         add_w4(second, 0, range(JQ))
 
-        turned = psum.tile([P, S], F32, name="second", tag="second")
+        turned = banks_at(6)[0]
         nc.tensor.transpose(turned[:, 0:P], bias_rows[:], identity[:])
         cast_w1(1, 0)
         nc.scalar.copy(bias[:], turned[:, 0:2 * MT])
@@ -210,26 +213,48 @@ def tile_list_derby_jam_lineups_kernel(tc, tab_words, tab_scales, offs, tab2_wor
         quantize(w1_q[1][0][:], w1_sc[1][0][:], w1_bf[1][0][:])
         gather_words(v2[0], tab2[0], idx2)
         quantize(w1_q[1][1][:], w1_sc[1][1][:], w1_bf[1][1][:])
-        quantize(h_q[0][:], h_sc[0][:], h_bf[0][:])
-        first, second = banks_of("first"), banks_of("second")
-        w1_pass(first, 1, 0)
-        w1_pass(first, 1, 1)
-        w4_pass(second, 1, 0)
-        w4_pass(second, 1, 1)
-        take_larger(first, 1)
         gather_words(v2[1], tab2[1], idx2)
-        add_w4(second, 1, range(JQ))
-        quantize(h_q[1][:], h_sc[1][:], h_bf[1][:])
+        quantize(h_q[0][:], h_sc[0][:], h_bf[0][:])
+        first, second = banks_at(0, 1, 2, 3), banks_at(4, 5)
+        w1_pass(first, 1, 0)
+        for jq in range(2):
+            for a in range(NPASS):
+                w4_pass(second, 1, a, [jq])
+        w1_pass(first, 1, 1)
+        for q in range(MT):
+            bank = banks_at(6 + q % 2)[0]
+            lineup_product(bank[:], q, v, v_sc, slice(0, S))
+            nc.scalar.activation(gate[q][:], bank[:], ACT.Tanh, bias=bias[:, q:q + 1])
+        for q in range(2):
+            nc.gpsimd.tensor_tensor(gate_w[q][:], gate[q][:], wgo_sb[:], ALU.mult)
+        take_larger(first, 1)
+        second = second + banks_at(0, 1)
+        for jq in range(2, JQ):
+            for a in range(NPASS):
+                w4_pass(second, 1, a, [jq])
 
-        first, second = banks_of("first"), banks_of("second")
-        for q in range(MT):
-            lineup_product(first[q][:], q, v, v_sc, slice(0, S))
-            nc.scalar.activation(gate[q][:], first[q][:], ACT.Tanh, bias=bias[:, q:q + 1])
-        for q in range(MT):
-            lineup_product(second[q][:], q, h_q, h_sc, slice(0, S))
-            nc.scalar.activation(score[q][:], second[q][:], ACT.Identity, bias=bias[:, MT + q:MT + q + 1])
-        for q in range(MT):
+        def quantize_half(u):
+            quantize(h_q[1][:, u * HALF:(u + 1) * HALF], h_sc[1][:, u * HALF:(u + 1) * HALF],
+                     h_bf[1][:, u * HALF * PACK:(u + 1) * HALF * PACK])
+
+        add_w4(second, 1, range(0, 3))
+        quantize_half(0)
+        add_w4(second, 1, range(3, 4))
+        quantize_half(1)
+        for q in range(2, MT):
             nc.vector.tensor_tensor(gate_w[q][:], gate[q][:], wgo_sb[:], ALU.mult)
-        for q in range(MT):
-            nc.vector.tensor_tensor(page[q][:].indirect(idx3[:]), score[q][:], gate_w[q][:], ALU.mult)
-            nc.sync.dma_start(out[q * P:(q + 1) * P, :], page[q][:])
+
+        for u in range(2):
+            jams = slice(u * HALF, (u + 1) * HALF)
+            banks = banks_at(2, 3, 6, 7) if u == 0 else banks_at(4, 5, 0, 1)
+            for q in range(MT):
+                lineup_product(banks[q][:, 0:HALF], q, h_q, h_sc, jams)
+                nc.scalar.activation(score[q][:, jams], banks[q][:, 0:HALF], ACT.Identity, bias=bias[:, MT + q:MT + q + 1])
+        for pair in range(MT // 2):
+            for u in range(2):
+                jams = slice(u * HALF, (u + 1) * HALF)
+                for q in (2 * pair, 2 * pair + 1):
+                    nc.vector.tensor_tensor(page[q][:].indirect(idx3[:, u * HALF // 16:(u + 1) * HALF // 16]),
+                                            score[q][:, jams], gate_w[q][:, jams], ALU.mult)
+                    if u == 1:
+                        nc.sync.dma_start(out[q * P:(q + 1) * P, :], page[q][:])

from contextlib import ExitStack

import concourse.mybir as mybir
from concourse.masks import make_identity

K, H, T, S, T3, S2, T2 = 1024, 1024, 2048, 512, 2048, 512, 1024
FLOPS = 2 * (2 * K * H * S + 2 * H * S2 * S)

F32 = mybir.dt.float32
BF16 = mybir.dt.bfloat16
I32 = mybir.dt.int32
U32 = mybir.dt.uint32
U16 = mybir.dt.uint16
U8 = mybir.dt.uint8
FP8X4 = mybir.dt.float8_e4m3fn_x4
FP4X4 = mybir.dt.float4_e2m1fn_x4
ALU = mybir.AluOpType
ACT = mybir.ActivationFunctionType

P = 128
PACK = 4
KP = P * PACK
NPASS = K // KP
NBLK = H // KP
MT = S2 // P
JQ = S // P
HALF = S // 2


def tile_list_derby_jam_lineups_kernel(tc, tab_words, tab_scales, offs, tab2_words, tab2_scales, offs2, offs3,
                                                 w1, w4_words, w4_scales, seen, ba, bt, wgo, page1, out):
    nc = tc.nc
    with ExitStack() as ctx:
        keep = ctx.enter_context(tc.tile_pool(name="keep", bufs=1))
        psum = ctx.enter_context(tc.psum_pool(name="psum", bufs=1))

        def held(name, shape, dtype):
            return keep.tile(shape, dtype, name=name, align_bytes=64)

        idx = keep.tile([P, S // 16], U16, name="idx")
        idx2 = keep.tile([P, S2 // 16], U16, name="idx2")
        idx3 = keep.tile([P, S // 16], U16, name="idx3")
        tab = [held("tab%d" % a, [P, T], I32) for a in range(NPASS)]
        tab2 = [held("tab2_%d" % a, [P, T3], I32) for a in range(NPASS)]
        tab_sc = held("tab_sc", [P, NPASS * T], U8)
        tab2_sc = held("tab2_sc", [P, T3], U8)
        w4_raw = held("w4_raw", [P, NPASS * 2 * H], U8)
        w4_sc_raw = held("w4_sc_raw", [P, NPASS * H], U8)
        w4 = held("w4", [P, NPASS * 2 * H], U8)
        w4_sc = held("w4_sc", [P, NPASS * H], U8)
        pieces = [[1, 1], [1, 2]]
        w1_raw = [[[held("w1_raw%d%d%d" % (b, a, u), [P, PACK, KP // pieces[b][a]], F32) for u in range(pieces[b][a])]
                   for a in range(NPASS)] for b in range(NBLK)]
        w1_bf = [[held("w1_bf%d%d" % (b, a), [P, KP * PACK], BF16) for a in range(NPASS)] for b in range(NBLK)]
        w1_q = [[held("w1_q%d%d" % (b, a), [P, KP], U32) for a in range(NPASS)] for b in range(NBLK)]
        w1_sc = [[held("w1_sc%d%d" % (b, a), [P, KP], U8) for a in range(NPASS)] for b in range(NBLK)]
        seen_sb = [[held("seen%d%d" % (b, u), [P, 2, S], F32) for u in range(2)] for b in range(NBLK)]
        v = [held("v%d" % a, [P, S], U32) for a in range(NPASS)]
        v_sc = [held("v_sc%d" % a, [P, S], U8) for a in range(NPASS)]
        v2 = [held("v2_%d" % a, [P, S2], U32) for a in range(NPASS)]
        v2_sc = held("v2_sc", [P, S2], U8)
        larger = [held("larger%d" % b, [P, 2, S, 2], F32) for b in range(NBLK)]
        h_bf = [held("h_bf%d" % b, [P, S * PACK], BF16) for b in range(NBLK)]
        h_q = [held("h_q%d" % b, [P, S], U32) for b in range(NBLK)]
        h_sc = [held("h_sc%d" % b, [P, S], U8) for b in range(NBLK)]
        bias_rows = held("bias_rows", [P, P], F32)
        identity = held("identity", [P, P], F32)
        bias = held("bias", [P, 2 * MT], F32)
        wgo_sb = held("wgo_sb", [P, S], F32)
        page = [held("page%d" % q, [P, T2], F32) for q in range(MT)]
        gate = [held("gate%d" % q, [P, S], F32) for q in range(MT)]
        gate_w = [held("gate_w%d" % q, [P, S], F32) for q in range(MT)]
        score = [held("score%d" % q, [P, S], F32) for q in range(MT)]

        def load_words(dst, words, a):
            nc.sync.dma_start(dst[a][:], words[a].rearrange("p t i -> p (t i)").bitcast(I32))

        def load_w1(b, a):
            width = KP // pieces[b][a]
            for u in range(pieces[b][a]):
                c0 = b * KP + u * width
                nc.sync.dma_start(w1_raw[b][a][u][:],
                                  w1[a * KP:(a + 1) * KP, c0:c0 + width].rearrange("(p i) c -> p i c", i=PACK))

        def load_seen(b, x):
            rows = seen[b * KP:(b + 1) * KP, :].rearrange("(p t) j -> p t j", t=PACK)
            nc.sync.dma_start(seen_sb[b][x][:], rows[:, 2 * x:2 * x + 2, :])

        def load_planes_side_by_side(queue, dst, scales):
            for quad in range(4):
                queue.dma_start(dst[32 * quad:32 * quad + 4, :].bitcast(I32).rearrange("r (a n) -> r a n", a=NPASS),
                                scales[:, 4 * quad:4 * quad + 4, :].bitcast(I32).rearrange("a r n -> r a n"))

        def cast_w1(b, a):
            width = P // pieces[b][a]
            dealt = w1_bf[b][a][:].rearrange("p (t m x y) -> p m x t y", t=PACK, x=2, y=2)
            for u in range(pieces[b][a]):
                nc.scalar.copy(dealt[:, u * width:(u + 1) * width],
                               w1_raw[b][a][u][:].rearrange("p (x y) (m t) -> p m x t y", y=2, t=PACK))

        def quantize(codes, scales, values):
            nc.vector.quantize_mx(out=codes.bitcast(FP8X4), scales=scales, in_=values)

        def gather_words(dst, src, offsets):
            nc.vector.tensor_copy(dst[:], src[:].bitcast(U32).indirect(offsets[:]))

        def w1_pass(banks, b, a):
            for x in range(2):
                for u in range(2):
                    jams = slice(u * HALF, (u + 1) * HALF)
                    for y in range(2):
                        cols = slice((2 * x + y) * P, (2 * x + y + 1) * P)
                        nc.tensor.matmul_mx(out=banks[2 * x + u][:, y * HALF:(y + 1) * HALF], lhsT=w1_q[b][a][:, cols].bitcast(FP8X4),
                                            lhsT_scale=w1_sc[b][a][:, cols], rhs=v[a][:, jams].bitcast(FP8X4),
                                            rhs_scale=v_sc[a][:, jams], start=(a == 0 and y == 0),
                                            stop=(a == NPASS - 1 and y == 1))

        def w4_pass(banks, b, a, quarters):
            for jq in quarters:
                jams = slice(jq * P, (jq + 1) * P)
                for t in range(PACK):
                    c0 = a * H + b * KP + t * P
                    nc.tensor.matmul_mx(out=banks[jq][:, t * P:(t + 1) * P], lhsT=w4[:, 2 * c0:2 * (c0 + P)].bitcast(FP4X4),
                                        lhsT_scale=w4_sc[:, c0:c0 + P], rhs=v[a][:, jams].bitcast(FP8X4),
                                        rhs_scale=v_sc[a][:, jams], start=(a == 0 and t == 0),
                                        stop=(a == NPASS - 1 and t == PACK - 1))

        def take_larger(banks, b):
            for x in range(2):
                for u in range(2):
                    jams = slice(u * HALF, (u + 1) * HALF)
                    nc.vector.tensor_tensor(larger[b][:, x, jams, :], banks[2 * x + u][:].rearrange("p (y j) -> p j y", y=2),
                                            seen_sb[b][x][:, :, jams].rearrange("p y j -> p j y"), ALU.max)

        def add_w4(banks, b, quarters):
            for jq in quarters:
                nc.vector.tensor_tensor(
                    h_bf[b][:, jq * KP:(jq + 1) * KP].rearrange("p (j x y) -> p j x y", x=2, y=2),
                    banks[jq][:].rearrange("p (x y j) -> p j x y", x=2, y=2),
                    larger[b][:, :, jq * P:(jq + 1) * P, :].rearrange("p x j y -> p j x y"), ALU.add)

        def lineup_product(bank, q, codes, scales, jams):
            cols = slice(q * P, (q + 1) * P)
            for a in range(NPASS):
                nc.tensor.matmul_mx(out=bank, lhsT=v2[a][:, cols].bitcast(FP8X4), lhsT_scale=v2_sc[8 + 4 * a:P, cols],
                                    rhs=codes[a][:, jams].bitcast(FP8X4), rhs_scale=scales[a][:, jams], start=(a == 0), stop=(a == NPASS - 1))

        def banks_at(*numbers):
            return [psum.tile([P, S], F32, name="bank%d" % n, tag="bank%d" % n) for n in numbers]

        nc.gpsimd.memset(w4_sc_raw[:].bitcast(I32), 0)
        nc.vector.memset(tab_sc[:].bitcast(I32), 0)
        nc.gpsimd.memset(tab2_sc[:].bitcast(I32), 0)
        nc.gpsimd.memset(bias_rows[:], 0.0)

        nc.sync.dma_start(w4_raw[:].bitcast(I32).rearrange("p (a n) -> p a n", a=NPASS),
                          w4_words.bitcast(I32).rearrange("a p n -> p a n"))
        nc.sync.dma_start(idx[:], offs)
        nc.sync.dma_start(idx3[:], offs3)
        load_planes_side_by_side(nc.sync, w4_sc_raw, w4_scales)
        load_w1(0, 0)
        nc.gpsimd.dma_start(bias_rows[0:MT, :], bt.rearrange("(q p) -> q p", p=P))
        nc.gpsimd.dma_start(bias_rows[MT:2 * MT, :], ba.rearrange("(q p) -> q p", p=P))
        load_planes_side_by_side(nc.sync, tab_sc, tab_scales)
        load_words(tab, tab_words, 0)
        load_w1(0, 1)
        for quad in range(4):
            nc.sync.dma_start(tab2_sc[32 * quad + 8:32 * quad + 16, :].bitcast(I32),
                              tab2_scales[:, 4 * quad:4 * quad + 4, :].bitcast(I32))
        nc.sync.dma_start(idx2[:], offs2)
        load_words(tab, tab_words, 1)
        load_seen(0, 0)
        load_seen(0, 1)
        load_w1(1, 0)
        load_words(tab2, tab2_words, 0)
        load_w1(1, 1)
        load_words(tab2, tab2_words, 1)
        load_seen(1, 0)
        nc.sync.dma_start(wgo_sb[:], wgo)
        load_seen(1, 1)
        for q in range(MT):
            nc.sync.dma_start(page[q][:], page1[q * P:(q + 1) * P, :])
        make_identity(nc, identity[:])

        nc.vector.tensor_copy(w4[:].bitcast(U16).rearrange("p (g t m) -> p g t m", t=PACK, m=P),
                              w4_raw[:].bitcast(U16).rearrange("p (g m t) -> p g t m", t=PACK, m=P))
        nc.vector.tensor_copy(w4_sc[:].rearrange("p (g t m) -> p g t m", t=PACK, m=P),
                              w4_sc_raw[:].rearrange("p (g m t) -> p g t m", t=PACK, m=P))
        for a in range(NPASS):
            nc.vector.tensor_copy(v_sc[a][:], tab_sc[:, a * T:(a + 1) * T].indirect(idx[:]))
        cast_w1(0, 0)
        cast_w1(0, 1)
        gather_words(v[0], tab[0], idx)
        quantize(w1_q[0][0][:], w1_sc[0][0][:], w1_bf[0][0][:])
        nc.vector.tensor_copy(v2_sc[:], tab2_sc[:].indirect(idx2[:]))
        quantize(w1_q[0][1][:], w1_sc[0][1][:], w1_bf[0][1][:])
        for u in range(2):
            nc.vector.tensor_copy(v[1][:, u * HALF:(u + 1) * HALF],
                                  tab[1][:].bitcast(U32).indirect(idx[:, u * HALF // 16:(u + 1) * HALF // 16]))
        first, second = banks_at(0, 1, 2, 3), banks_at(4, 5, 6, 7)
        w1_pass(first, 0, 0)
        w4_pass(second, 0, 0, range(JQ))
        w1_pass(first, 0, 1)
        w4_pass(second, 0, 1, range(JQ))
        take_larger(first, 0)
        add_w4(second, 0, range(JQ))

        turned = banks_at(6)[0]
        nc.tensor.transpose(turned[:, 0:P], bias_rows[:], identity[:])
        cast_w1(1, 0)
        nc.scalar.copy(bias[:], turned[:, 0:2 * MT])
        cast_w1(1, 1)
        quantize(w1_q[1][0][:], w1_sc[1][0][:], w1_bf[1][0][:])
        gather_words(v2[0], tab2[0], idx2)
        quantize(w1_q[1][1][:], w1_sc[1][1][:], w1_bf[1][1][:])
        gather_words(v2[1], tab2[1], idx2)
        quantize(h_q[0][:], h_sc[0][:], h_bf[0][:])
        first, second = banks_at(0, 1, 2, 3), banks_at(4, 5)
        w1_pass(first, 1, 0)
        for jq in range(2):
            for a in range(NPASS):
                w4_pass(second, 1, a, [jq])
        w1_pass(first, 1, 1)
        for q in range(MT):
            bank = banks_at(6 + q % 2)[0]
            lineup_product(bank[:], q, v, v_sc, slice(0, S))
            nc.scalar.activation(gate[q][:], bank[:], ACT.Tanh, bias=bias[:, q:q + 1])
        for q in range(2):
            nc.gpsimd.tensor_tensor(gate_w[q][:], gate[q][:], wgo_sb[:], ALU.mult)
        take_larger(first, 1)
        second = second + banks_at(0, 1)
        for jq in range(2, JQ):
            for a in range(NPASS):
                w4_pass(second, 1, a, [jq])

        def quantize_half(u):
            quantize(h_q[1][:, u * HALF:(u + 1) * HALF], h_sc[1][:, u * HALF:(u + 1) * HALF],
                     h_bf[1][:, u * HALF * PACK:(u + 1) * HALF * PACK])

        add_w4(second, 1, range(0, 3))
        quantize_half(0)
        add_w4(second, 1, range(3, 4))
        quantize_half(1)
        for q in range(2, MT):
            nc.vector.tensor_tensor(gate_w[q][:], gate[q][:], wgo_sb[:], ALU.mult)

        for u in range(2):
            jams = slice(u * HALF, (u + 1) * HALF)
            banks = banks_at(2, 3, 6, 7) if u == 0 else banks_at(4, 5, 0, 1)
            for q in range(MT):
                lineup_product(banks[q][:, 0:HALF], q, h_q, h_sc, jams)
                nc.scalar.activation(score[q][:, jams], banks[q][:, 0:HALF], ACT.Identity, bias=bias[:, MT + q:MT + q + 1])
        for pair in range(MT // 2):
            for u in range(2):
                jams = slice(u * HALF, (u + 1) * HALF)
                for q in (2 * pair, 2 * pair + 1):
                    nc.vector.tensor_tensor(page[q][:].indirect(idx3[:, u * HALF // 16:(u + 1) * HALF // 16]),
                                            score[q][:, jams], gate_w[q][:, jams], ALU.mult)
                    if u == 1:
                        nc.sync.dma_start(out[q * P:(q + 1) * P, :], page[q][:])
